import numpy as np, ml_dtypes
CORES = [3,7,11,15,131,135,139,143]
N = 8
TK = 64
def gelu(z): return 0.5 * z * (1.0 + np.tanh(0.7978845608028654 * (z + 0.044715 * z ** 3)))
def setup_inputs(rng):
    return {"x": rng.standard_normal((N, 128, TK), dtype=np.float32).astype(ml_dtypes.bfloat16), "w1": (rng.standard_normal((N, 128, 128), dtype=np.float32) / 8).astype(ml_dtypes.bfloat16), "w2": (rng.standard_normal((N, 128, 128), dtype=np.float32) / 8).astype(ml_dtypes.bfloat16)}
def setup_inputs_big(rng):
    d = setup_inputs(rng)
    for k in ("x",): d[k] = (d[k].astype(np.float32) * 1024.0).astype(d[k].dtype)
    return d
def setup_inputs_small(rng):
    d = setup_inputs(rng)
    for k in ("x",): d[k] = (d[k].astype(np.float32) * (1 / 1024.0)).astype(d[k].dtype)
    return d
def setup_inputs_apart(rng):
    d = setup_inputs(rng)
    f = (10.0 ** rng.permutation(np.linspace(-1.5, 1.5, N))).astype(np.float32).reshape(N, 1, 1)
    for k in ("x",): d[k] = (d[k].astype(np.float32) * f).astype(d[k].dtype)
    return d
def reference(x, w1, w2):
    X, W1, W2 = x.astype(np.float64), w1.astype(np.float64), w2.astype(np.float64)
    y = np.zeros((N, 128, TK))
    for r in range(N):
        for j in range(N):
            y[r] += W2[j].T @ (gelu(W1[j].T @ X[r]))
    return {"y": y.astype(ml_dtypes.bfloat16)}

from concourse.bass import DstId, RemoteDMATransfer
from concourse.mybir import AluOpType, ActivationFunctionType

P = 128
TK = 64
WW = 2 * P
BANK = 512
NBANK = 4

WAVES = (("plane_s", "diag_s"), ("mate_s", "mate_o"))
SHARED = ("plane_s", "diag_s")
ORDER = ("w0", "x", "w1")
FOLD = len(SHARED) > 0
CHIP_W = not FOLD

ROLES = (("chip_o",) if CHIP_W else ()) + tuple(r for w in WAVES for r in w)
SLOT = {"own": 0}
for _r in ROLES:
    SLOT[_r] = len(SLOT)


def _groups():
    gs = [[("own", 0)]]
    if FOLD:
        gs.append([("own", 1)])
    if CHIP_W:
        gs.append([("chip_o", 0)])
    for w in WAVES:
        sh = [(r, 1) for r in w if r in SHARED]
        if sh:
            gs.append(sh)
        gs.append([(r, 0) for r in w])
    return gs


GROUPS = _groups()
JOBS = [job for grp in GROUPS for job in grp]

SCRATCH = {
    "xb": ("sbuf", [P, 2 * TK], "bfloat16"),
    "wall": ("sbuf", [P, len(SLOT) * WW], "bfloat16"),
    "hs": ("sbuf", [P, len(JOBS) * TK], "bfloat16"),
    "ysend": ("sbuf", [P, TK], "bfloat16"),
    "yland": ("sbuf", [P, TK], "bfloat16"),
    "yout": ("sbuf", [P, TK], "bfloat16"),
    "acc0": ("psum", [P, BANK], "float32"),
    "acc1": ("psum", [P, BANK], "float32"),
}
for _b in range(NBANK):
    SCRATCH["hp%d" % _b] = ("psum", [P, BANK], "float32")

SEMAPHORES = (["wl", "xl", "ax", "ay", "ls", "cp", "fin", "st", "d0", "d1"] + ["a_" + r for r in ROLES]
              + ["m%d" % j for j in range(len(JOBS))] + ["g%d" % j for j in range(len(JOBS))])


def _role(topo, me, q):
    if topo.host(me) == topo.host(q) and topo.chip(me) == topo.chip(q):
        place = "chip"
    elif topo.mates(me, q):
        place = "mate"
    elif topo.same_plane(me, q):
        place = "plane"
    else:
        place = "diag"
    return place + ("_s" if topo.die(me) == topo.die(q) else "_o")


def _bits(m):
    return [b for b in range(m.bit_length()) if (m >> b) & 1]


def _mask(bits):
    return sum(1 << b for b in bits)


def rank_program(g, core, T, topo):
    if T.rank_of(core) is None:
        return
    S = T.sem
    te, sc, ve, sy = g.tensor, g.scalar, g.vector, g.sync
    peers = {}
    for q in T.cores:
        if q != core:
            peers[_role(topo, core, q)] = q
    partner = peers["chip_o"]
    far = topo.mask(core, partner)
    for w in WAVES:
        for r in w:
            assert topo.may_write(core, peers[r])
            far &= topo.mask(core, peers[r])
    far_eng = _bits(far)
    near_eng = _bits(topo.mask(core, partner) & ~far)
    n_of = {"chip_o": len(near_eng)}
    for w in WAVES:
        for r in w:
            n_of[r] = len(far_eng) // len(w)
    sent = [0]

    def wslot(r):
        return T.wall[:, SLOT[r] * WW:(SLOT[r] + 1) * WW]

    sy.dma_start(T.wall[:, 0:P], T.w1[:]).then_inc(S.wl, 16)
    sc.dma_start(T.wall[:, P:WW], T.w2[:]).then_inc(S.wl, 16)
    sy.dma_start(T.xb[:, 0:TK], T.x[:]).then_inc(S.xl, 16)

    def near_write(out_ap, in_ap, sem):
        rid, pid = topo.addr(partner, core)
        g.remote_dma(out_ap=out_ap, in_ap=in_ap, remote_sem=sem, local_sem=S.ls, pid=pid, routing_id=rid,
                     dma_engine_mask=_mask(near_eng))
        sent[0] += len(near_eng)

    g.wait_ge(S.wl, 32)
    for step in ORDER:
        if step == "x":
            g.wait_ge(S.xl, 16)
            near_write(T.xb[:, TK:2 * TK], T.xb[:, 0:TK], S.ax)
        elif step == "c":
            near_write(wslot("chip_o"), wslot("own"), S["a_chip_o"])
        else:
            wave = WAVES[int(step[1:])]
            trs = []
            for i, r in enumerate(wave):
                n = n_of[r]
                rid, pid = topo.addr(peers[r], core)
                trs.append(RemoteDMATransfer(dst_ids=[DstId(rid=rid, pnc=pid)], dma_engine_mask=_mask(far_eng[i * n:(i + 1) * n]),
                                             remote_sem=S["a_" + r], src=wslot("own"), dst=wslot(r)))
                sent[0] += n
            g.remote_dma_fused(trs, local_sem=S.ls)

    acc = (T.acc0, T.acc1)
    total = [sum(1 for _, t in JOBS if t == k) for k in (0, 1)]
    seen = [0, 0]
    waited = {}

    def need(sem, n):
        if sem not in waited:
            te.wait_ge(S[sem], n)
            waited[sem] = n

    j = 0
    for grp in GROUPS:
        first = j
        for r, t in grp:
            if r == "own":
                need("wl", 32)
            else:
                need("a_" + r, n_of[r])
            if t == 0:
                need("xl", 16)
            else:
                need("ax", len(near_eng))
            hp = T["hp%d" % (j % NBANK)][:, 0:TK]
            w0 = SLOT[r] * WW
            te.matmul(hp, T.wall[:, w0:w0 + P], T.xb[:, t * TK:(t + 1) * TK], True, True).then_inc(S["m%d" % j], 1)
            sc.wait_ge(S["m%d" % j], 1)
            sc.activation(T.hs[:, j * TK:(j + 1) * TK], hp, ActivationFunctionType.Gelu_apprx_tanh).then_inc(S["g%d" % j], 1)
            j += 1
        j = first
        for r, t in grp:
            w0 = SLOT[r] * WW + P
            te.wait_ge(S["g%d" % j], 1)
            te.matmul(acc[t][:, 0:TK], T.wall[:, w0:w0 + P], T.hs[:, j * TK:(j + 1) * TK], seen[t] == 0,
                      seen[t] == total[t] - 1).then_inc(S["d%d" % t], 1)
            seen[t] += 1
            j += 1

    if FOLD:
        ve.wait_ge(S.d1, total[1])
        ve.tensor_copy(T.ysend[:], T.acc1[:, 0:TK]).then_inc(S.cp, 1)
        g.wait_ge(S.cp, 1)
        near_write(T.yland[:], T.ysend[:], S.ay)
        ve.wait_ge(S.d0, total[0])
        ve.wait_ge(S.ay, len(near_eng))
        ve.tensor_tensor(T.yout[:], T.acc0[:, 0:TK], T.yland[:], AluOpType.add).then_inc(S.fin, 1)
    else:
        ve.wait_ge(S.d0, total[0])
        ve.tensor_copy(T.yout[:], T.acc0[:, 0:TK]).then_inc(S.fin, 1)
    sy.wait_ge(S.fin, 1)
    sy.dma_start(T.y[:], T.yout[:]).then_inc(S.st, 16)
    sy.wait_ge(S.st, 16)
    g.wait_ge(S.ls, sent[0])
